import numpy as np
import ml_dtypes


def mxq(x, axis, fmt="e4m3"):
    dtype, down = {"e4m3": (ml_dtypes.float8_e4m3fn, 7), "e5m2": (ml_dtypes.float8_e5m2, 14)}[fmt]
    v = np.moveaxis(np.asarray(x, np.float32).astype(ml_dtypes.bfloat16).astype(np.float64), axis, -1)
    blocks = v.reshape(v.shape[:-1] + (-1, 32))
    amax = np.abs(blocks).max(-1, keepdims=True)
    byte = np.maximum(np.where(amax > 0, np.frexp(amax)[1] - 1 + 127, 0) - down, 1)
    scale = np.exp2(byte - 127.0)
    codes = (blocks / scale).astype(np.float32).astype(dtype).astype(np.float64)
    return np.moveaxis((codes * scale).reshape(v.shape), -1, axis)


WIDE = False


def mx_kscale(k):
    if not WIDE:
        return np.ones(k)
    levels = np.array([10, -10, 5, -5, 0])
    if k % 512:
        return np.exp2(np.random.permutation(np.resize(levels, k // 32))).repeat(32)
    a = np.empty((k // 512, 16))
    for p in range(k // 512):
        a[p, :8] = np.random.permutation(np.resize(levels, 8))
        for g in range(8):
            far = levels[np.abs(levels - a[p, g]) >= 10]
            a[p, g + 8] = far[np.random.randint(len(far))]
    return np.exp2(a.ravel()).repeat(32)


def f64(x):
    return np.asarray(x).astype(np.float64)


def striped(idx):
    return np.tile(idx.reshape(-1, 16).T, (8, 1)).astype(np.uint16)


def unstriped(offs):
    return offs[:16].T.reshape(-1).astype(np.int64)


def pack_weight(w):
    k, n = w.shape
    w = f64(np.asarray(w, np.float32).astype(ml_dtypes.bfloat16)).reshape(k // 32, 32, n)
    amax = np.abs(w).max(1)
    byte = np.clip(np.where(amax > 0, np.frexp(amax)[1] - 1 + 127 - 7, 1), 1, 254)
    scaled = (w * np.exp2(127.0 - byte)[:, None, :]).reshape(k, n).astype(np.float32)
    words = np.ascontiguousarray(scaled.reshape(k // 512, 128, 4, n).transpose(0, 1, 3, 2)).astype(ml_dtypes.float8_e4m3fn).view(np.uint8)
    return words, np.ascontiguousarray(byte.astype(np.uint8).reshape(k // 512, 16, n))


def unpack_weight(words, scales):
    g, p, n, _ = words.shape
    vals = np.ascontiguousarray(words).view(ml_dtypes.float8_e4m3fn).astype(np.float64) * np.repeat(np.exp2(scales.astype(np.float64) - 127.0), 8, axis=1)[..., None]
    return vals.transpose(0, 1, 3, 2).reshape(g * 512, n)


K, T, N = 2048, 256, 256


def setup_inputs():
    n = np.random.standard_normal
    s = mx_kscale(K)[:, None]
    idx = np.random.permutation(K)
    x = n((T, K))
    x[:, idx] *= s[:, 0]
    words, scales = pack_weight(n((K, N)) / np.sqrt(K) / s)
    return {
        "x": x.astype(np.float32),
        "w_words": words,
        "w_scales": scales,
        "b": (0.3 * n((N, 1))).astype(np.float32),
        "offs": striped(idx),
    }


def reference(x, w_words, w_scales, b, offs):
    w = unpack_weight(w_words, w_scales)
    idx = unstriped(offs)
    xq = mxq(f64(x)[:, idx], 1, "e4m3").T
    return (w.T @ xq) + f64(b)

@@ -1,0 +1,189 @@
+from contextlib import ExitStack
+
+import concourse.mybir as mybir
+from concourse.masks import make_identity
+
+F32 = mybir.dt.float32
+BF16 = mybir.dt.bfloat16
+I32 = mybir.dt.int32
+U32 = mybir.dt.uint32
+U16 = mybir.dt.uint16
+U8 = mybir.dt.uint8
+FP8X4 = mybir.dt.float8_e4m3fn_x4
+COPY = mybir.ActivationFunctionType.Copy
+IDENTITY = mybir.ActivationFunctionType.Identity
+ADD = mybir.AluOpType.add
+
+K, T, N = 2048, 256, 256
+P = 128
+PASSES = 4
+FLOPS = 2 * K * T * N
+
+
+def tile_picked_actorder_lin_bias_perm_l_kernel(tc, x, w_words, w_scales, b, offs, out):
+    nc = tc.nc
+    with ExitStack() as ctx:
+        keep = ctx.enter_context(tc.tile_pool(name="keep", bufs=1))
+        ring = ctx.enter_context(tc.tile_pool(name="ring", bufs=4))
+        turned = ctx.enter_context(tc.psum_pool(name="turned", bufs=4))
+        sums = ctx.enter_context(tc.psum_pool(name="sums", bufs=1))
+
+        offsets = keep.tile([P, K // 16], U16, name="offsets")
+        x32 = [keep.tile([P, K], F32, name="x32_%d" % h) for h in range(2)]
+        x16 = [keep.tile([P, K], BF16, name="x16_%d" % h) for h in range(2)]
+        w_codes = keep.tile([P, PASSES, N], U32, name="w_codes", align_bytes=64)
+        w_planes = keep.tile([P, N], U8, name="w_planes", align_bytes=64)
+        x_codes = keep.tile([P, PASSES, T], U32, name="x_codes", align_bytes=64)
+        x_planes = keep.tile([P, PASSES, T], U8, name="x_planes", align_bytes=64)
+        b_rows = keep.tile([P, P], F32, name="b_rows")
+        bias = keep.tile([P, 2], F32, name="bias")
+        ident = keep.tile([P, P], F32, name="ident")
+
+        def load_x(h, lo, hi):
+            nc.sync.dma_start(x32[h][:, lo:hi], x[P * h : P * h + P, lo:hi])
+
+        make_identity(nc, ident[:])
+        nc.vector.memset(w_planes[:].bitcast(I32), 0)
+        nc.vector.memset(b_rows[:], 0.0)
+
+        load_x(0, 0, 512)
+        load_x(0, 512, 1024)
+        nc.sync.dma_start(offsets[:], offs)
+        load_x(0, 1024, 1536)
+        load_x(0, 1536, 2048)
+        for c in range(4):
+            load_x(1, 512 * c, 512 * c + 512)
+        nc.sync.dma_start(w_codes[:].bitcast(I32), w_words.rearrange("a p n t -> p a (n t)").bitcast(I32))
+        for q in range(4):
+            nc.sync.dma_start(
+                w_planes[32 * q : 32 * q + 16, :].bitcast(I32), w_scales[:, 4 * q : 4 * q + 4, :].bitcast(I32)
+            )
+        nc.gpsimd.dma_start(b_rows[0:2, :], b.rearrange("(c p) o -> c (p o)", p=P))
+
+        acc = [[sums.tile([P, P], F32, name="acc_%d_%d" % (h, m)) for m in range(2)] for h in range(2)]
+        gathered = {}
+        words = {}
+        grouped = {}
+        seen = [0, 0]
+
+        def cast(h, lo, hi, engine):
+            if engine == "v":
+                nc.vector.tensor_copy(x16[h][:, lo:hi], x32[h][:, lo:hi])
+            else:
+                nc.scalar.copy(x16[h][:, lo:hi], x32[h][:, lo:hi])
+
+        def gather(h, a, engine):
+            g = ring.tile([P, 2, 256], BF16, name="g", align_bytes=64)
+            gathered[h, a] = g
+            dst = g[:].rearrange("p u (j e) -> p j u e", e=2)
+            picks = offsets[:, 32 * a : 32 * a + 32]
+            if engine == "v":
+                nc.vector.tensor_copy(dst, x32[h][:].indirect(picks))
+            else:
+                nc.scalar.activation(dst, x16[h][:].indirect(picks), COPY)
+
+        def turn(h, a):
+            w = turned.tile([P, 4, P], F32, name="xt")
+            words[h, a] = w
+            pairs = gathered[h, a][:].rearrange("p u w -> p (u w)").bitcast(F32)
+            for u in range(2):
+                nc.tensor.transpose(w[:, u, :], pairs[:, P * u : P * u + P], ident[:])
+
+        def regroup(h, a, engine):
+            q = ring.tile([P, 4 * P], BF16, name="q", align_bytes=64)
+            grouped[h, a] = q
+            dst = q[:].bitcast(F32).rearrange("p (r u) -> p r u", u=2)
+            src = words[h, a][:, 0:2, :].rearrange("p u r -> p r u")
+            if engine == "v":
+                nc.vector.tensor_copy(dst, src)
+            else:
+                nc.scalar.copy(dst, src)
+
+        def quant(h, a):
+            cols = slice(P * h, P * h + P)
+            nc.vector.quantize_mx(
+                out=x_codes[:, a, cols].bitcast(FP8X4), scales=x_planes[:, a, cols], in_=grouped[h, a][:]
+            )
+
+        def mult(h, a):
+            cols = slice(P * h, P * h + P)
+            for m in range(2):
+                rows = slice(P * m, P * m + P)
+                nc.tensor.matmul_mx(
+                    out=acc[h][m][:],
+                    lhsT=w_codes[:, a, rows].bitcast(FP8X4),
+                    lhsT_scale=w_planes[4 * a : P, rows],
+                    rhs=x_codes[:, a, cols].bitcast(FP8X4),
+                    rhs_scale=x_planes[:, a, cols],
+                    start=(seen[h] == 0),
+                    stop=(seen[h] == PASSES - 1),
+                )
+            seen[h] += 1
+
+        def bias_in(engine):
+            bt = turned.tile([P, 4, P], F32, name="xt")
+            nc.tensor.transpose(bt[:, 0, :], b_rows[:], ident[:])
+            if engine == "v":
+                nc.vector.tensor_copy(bias[:], bt[:, 0, 0:2])
+            else:
+                nc.scalar.copy(bias[:], bt[:, 0, 0:2])
+
+        def store(h, m, engine, queue):
+            o = ring.tile([P, P], F32, name="o")
+            if engine == "v":
+                nc.vector.tensor_scalar(o[:], acc[h][m][:], bias[:, m : m + 1], None, ADD)
+            else:
+                nc.scalar.activation(o[:], acc[h][m][:], IDENTITY, bias=bias[:, m : m + 1])
+            queue.dma_start(out[P * m : P * m + P, P * h : P * h + P], o[:])
+
+        cast(0, 0, 512, "s")
+        cast(0, 512, 1024, "s")
+        cast(0, 1024, 1536, "s")
+        cast(0, 1536, 2048, "v")
+        gather(0, 3, "v")
+        gather(0, 0, "s")
+        bias_in("v")
+        for c in range(4):
+            cast(1, 512 * c, 512 * c + 512, "v")
+        turn(0, 3)
+        regroup(0, 3, "v")
+        gather(0, 1, "s")
+        turn(0, 0)
+        regroup(0, 0, "s")
+        quant(0, 3)
+        gather(1, 0, "v")
+        mult(0, 3)
+        quant(0, 0)
+        mult(0, 0)
+        gather(0, 2, "s")
+        turn(0, 1)
+        regroup(0, 1, "s")
+        turn(1, 0)
+        gather(1, 1, "v")
+        quant(0, 1)
+        mult(0, 1)
+        gather(1, 3, "s")
+        turn(0, 2)
+        regroup(0, 2, "s")
+        regroup(1, 0, "s")
+        gather(1, 2, "v")
+        quant(0, 2)
+        mult(0, 2)
+        turn(1, 1)
+        regroup(1, 1, "s")
+        quant(1, 0)
+        mult(1, 0)
+        store(0, 0, "s", nc.sync)
+        store(0, 1, "s", nc.sync)
+        turn(1, 3)
+        regroup(1, 3, "s")
+        quant(1, 1)
+        mult(1, 1)
+        turn(1, 2)
+        regroup(1, 2, "v")
+        quant(1, 3)
+        mult(1, 3)
+        quant(1, 2)
+        mult(1, 2)
+        store(1, 0, "v", nc.sync)
+        store(1, 1, "s", nc.scalar)

@@ -13,6 +13,7 @@ FP8X4 = mybir.dt.float8_e4m3fn_x4
 COPY = mybir.ActivationFunctionType.Copy
 IDENTITY = mybir.ActivationFunctionType.Identity
 ADD = mybir.AluOpType.add
+MULT = mybir.AluOpType.mult
 
 K, T, N = 2048, 256, 256
 P = 128
@@ -24,7 +25,7 @@ def tile_picked_actorder_lin_bias_perm_l_kernel(tc, x, w_words, w_scales, b, off
     nc = tc.nc
     with ExitStack() as ctx:
         keep = ctx.enter_context(tc.tile_pool(name="keep", bufs=1))
-        ring = ctx.enter_context(tc.tile_pool(name="ring", bufs=4))
+        ring = ctx.enter_context(tc.tile_pool(name="ring", bufs=8))
         turned = ctx.enter_context(tc.psum_pool(name="turned", bufs=4))
         sums = ctx.enter_context(tc.psum_pool(name="sums", bufs=1))
 
@@ -33,9 +34,6 @@ def tile_picked_actorder_lin_bias_perm_l_kernel(tc, x, w_words, w_scales, b, off
         x16 = [keep.tile([P, K], BF16, name="x16_%d" % h) for h in range(2)]
         w_codes = keep.tile([P, PASSES, N], U32, name="w_codes", align_bytes=64)
         w_planes = keep.tile([P, N], U8, name="w_planes", align_bytes=64)
-        x_codes = keep.tile([P, PASSES, T], U32, name="x_codes", align_bytes=64)
-        x_planes = keep.tile([P, PASSES, T], U8, name="x_planes", align_bytes=64)
-        b_rows = keep.tile([P, P], F32, name="b_rows")
         bias = keep.tile([P, 2], F32, name="bias")
         ident = keep.tile([P, P], F32, name="ident")
 
@@ -44,31 +42,34 @@ def tile_picked_actorder_lin_bias_perm_l_kernel(tc, x, w_words, w_scales, b, off
 
         make_identity(nc, ident[:])
         nc.vector.memset(w_planes[:].bitcast(I32), 0)
-        nc.vector.memset(b_rows[:], 0.0)
 
         load_x(0, 0, 512)
         load_x(0, 512, 1024)
         nc.sync.dma_start(offsets[:], offs)
         load_x(0, 1024, 1536)
         load_x(0, 1536, 2048)
-        for c in range(4):
-            load_x(1, 512 * c, 512 * c + 512)
+        load_x(1, 0, 2048)
         nc.sync.dma_start(w_codes[:].bitcast(I32), w_words.rearrange("a p n t -> p a (n t)").bitcast(I32))
         for q in range(4):
             nc.sync.dma_start(
                 w_planes[32 * q : 32 * q + 16, :].bitcast(I32), w_scales[:, 4 * q : 4 * q + 4, :].bitcast(I32)
             )
-        nc.gpsimd.dma_start(b_rows[0:2, :], b.rearrange("(c p) o -> c (p o)", p=P))
+        nc.sync.dma_start(bias[:], b.rearrange("(c p) o -> p (c o)", p=P))
 
         acc = [[sums.tile([P, P], F32, name="acc_%d_%d" % (h, m)) for m in range(2)] for h in range(2)]
         gathered = {}
+        place = {}
         words = {}
         grouped = {}
+        codes = {}
+        planes = {}
         seen = [0, 0]
 
         def cast(h, lo, hi, engine):
             if engine == "v":
                 nc.vector.tensor_copy(x16[h][:, lo:hi], x32[h][:, lo:hi])
+            elif engine == "g":
+                nc.gpsimd.tensor_scalar(x16[h][:, lo:hi], x32[h][:, lo:hi], 1.0, 0.0, MULT, ADD)
             else:
                 nc.scalar.copy(x16[h][:, lo:hi], x32[h][:, lo:hi])
 
@@ -82,51 +83,57 @@ def tile_picked_actorder_lin_bias_perm_l_kernel(tc, x, w_words, w_scales, b, off
             else:
                 nc.scalar.activation(dst, x16[h][:].indirect(picks), COPY)
 
+        groups = {(1, 1): [(1, 1)], (1, 2): [(1, 2), (0, 3)], (0, 2): [(0, 2)], (0, 1): [(0, 1), (0, 0)], (1, 0): [(1, 0)], (1, 3): [(1, 3)]}
+        for lead, members in groups.items():
+            for i, unit in enumerate(members):
+                place[unit] = (lead, i)
+
         def turn(h, a):
-            w = turned.tile([P, 4, P], F32, name="xt")
-            words[h, a] = w
+            lead, i = place[h, a]
+            if lead not in words:
+                w = turned.tile([P, 2, 2, P], F32, name="xt")
+                words[lead] = w
             pairs = gathered[h, a][:].rearrange("p u w -> p (u w)").bitcast(F32)
             for u in range(2):
-                nc.tensor.transpose(w[:, u, :], pairs[:, P * u : P * u + P], ident[:])
+                nc.tensor.transpose(words[lead][:, i, u, :], pairs[:, P * u : P * u + P], ident[:])
 
         def regroup(h, a, engine):
-            q = ring.tile([P, 4 * P], BF16, name="q", align_bytes=64)
+            n = len(groups[h, a])
+            q = ring.tile([P, n, 4 * P], BF16, name="q%d" % n, align_bytes=64)
             grouped[h, a] = q
-            dst = q[:].bitcast(F32).rearrange("p (r u) -> p r u", u=2)
-            src = words[h, a][:, 0:2, :].rearrange("p u r -> p r u")
+            dst = q[:].rearrange("p n w -> p (n w)").bitcast(F32).rearrange("p (n r u) -> p n r u", n=n, u=2)
+            src = words[h, a][:, 0:n, :, :].rearrange("p n u r -> p n r u")
             if engine == "v":
                 nc.vector.tensor_copy(dst, src)
             else:
                 nc.scalar.copy(dst, src)
 
         def quant(h, a):
-            cols = slice(P * h, P * h + P)
+            n = len(groups[h, a])
+            c = ring.tile([P, n, P], U32, name="codes%d" % n, align_bytes=64)
+            s = ring.tile([P, n, P], U8, name="planes%d" % n, align_bytes=64)
+            codes[h, a] = c
+            planes[h, a] = s
             nc.vector.quantize_mx(
-                out=x_codes[:, a, cols].bitcast(FP8X4), scales=x_planes[:, a, cols], in_=grouped[h, a][:]
+                out=c[:].rearrange("p n r -> p (n r)").bitcast(FP8X4),
+                scales=s[:].rearrange("p n r -> p (n r)"),
+                in_=grouped[h, a][:].rearrange("p n w -> p (n w)"),
             )
 
         def mult(h, a):
-            cols = slice(P * h, P * h + P)
+            lead, i = place[h, a]
             for m in range(2):
                 rows = slice(P * m, P * m + P)
                 nc.tensor.matmul_mx(
                     out=acc[h][m][:],
                     lhsT=w_codes[:, a, rows].bitcast(FP8X4),
                     lhsT_scale=w_planes[4 * a : P, rows],
-                    rhs=x_codes[:, a, cols].bitcast(FP8X4),
-                    rhs_scale=x_planes[:, a, cols],
+                    rhs=codes[lead][:, i, :].bitcast(FP8X4),
+                    rhs_scale=planes[lead][:, i, :],
                     start=(seen[h] == 0),
                     stop=(seen[h] == PASSES - 1),
                 )
             seen[h] += 1
-
-        def bias_in(engine):
-            bt = turned.tile([P, 4, P], F32, name="xt")
-            nc.tensor.transpose(bt[:, 0, :], b_rows[:], ident[:])
-            if engine == "v":
-                nc.vector.tensor_copy(bias[:], bt[:, 0, 0:2])
-            else:
-                nc.scalar.copy(bias[:], bt[:, 0, 0:2])
 
         def store(h, m, engine, queue):
             o = ring.tile([P, P], F32, name="o")
@@ -136,54 +143,47 @@ def tile_picked_actorder_lin_bias_perm_l_kernel(tc, x, w_words, w_scales, b, off
                 nc.scalar.activation(o[:], acc[h][m][:], IDENTITY, bias=bias[:, m : m + 1])
             queue.dma_start(out[P * m : P * m + P, P * h : P * h + P], o[:])
 
-        cast(0, 0, 512, "s")
+        cast(0, 0, 512, "v")
         cast(0, 512, 1024, "s")
-        cast(0, 1024, 1536, "s")
-        cast(0, 1536, 2048, "v")
+        cast(0, 1024, 1536, "v")
         gather(0, 3, "v")
-        gather(0, 0, "s")
-        bias_in("v")
-        for c in range(4):
-            cast(1, 512 * c, 512 * c + 512, "v")
-        turn(0, 3)
-        regroup(0, 3, "v")
+        cast(0, 1536, 2048, "s")
         gather(0, 1, "s")
-        turn(0, 0)
-        regroup(0, 0, "s")
-        quant(0, 3)
-        gather(1, 0, "v")
-        mult(0, 3)
-        quant(0, 0)
-        mult(0, 0)
+        turn(0, 3)
         gather(0, 2, "s")
+        gather(1, 0, "v")
         turn(0, 1)
-        regroup(0, 1, "s")
-        turn(1, 0)
-        gather(1, 1, "v")
-        quant(0, 1)
-        mult(0, 1)
-        gather(1, 3, "s")
-        turn(0, 2)
-        regroup(0, 2, "s")
-        regroup(1, 0, "s")
+        gather(0, 0, "s")
         gather(1, 2, "v")
-        quant(0, 2)
-        mult(0, 2)
-        turn(1, 1)
-        regroup(1, 1, "s")
-        quant(1, 0)
-        mult(1, 0)
-        store(0, 0, "s", nc.sync)
-        store(0, 1, "s", nc.sync)
-        turn(1, 3)
-        regroup(1, 3, "s")
-        quant(1, 1)
-        mult(1, 1)
+        turn(0, 2)
+        turn(1, 0)
+        gather(1, 3, "v")
+        regroup(1, 0, "s")
+        turn(0, 0)
+        regroup(0, 2, "s")
+        regroup(0, 1, "s")
         turn(1, 2)
-        regroup(1, 2, "v")
-        quant(1, 3)
-        mult(1, 3)
+        gather(1, 1, "v")
+        turn(1, 3)
+        regroup(1, 2, "s")
+        regroup(1, 3, "s")
+        quant(0, 1)
+        turn(1, 1)
         quant(1, 2)
+        mult(0, 0)
+        mult(0, 1)
+        quant(0, 2)
+        regroup(1, 1, "s")
         mult(1, 2)
+        quant(1, 3)
+        mult(0, 3)
+        quant(1, 0)
+        mult(0, 2)
+        quant(1, 1)
+        mult(1, 3)
+        mult(1, 0)
+        store(0, 0, "v", nc.sync)
+        store(0, 1, "s", nc.scalar)
+        mult(1, 1)
         store(1, 0, "v", nc.sync)
         store(1, 1, "s", nc.scalar)

from contextlib import ExitStack

import concourse.mybir as mybir
from concourse.masks import make_identity

F32 = mybir.dt.float32
BF16 = mybir.dt.bfloat16
I32 = mybir.dt.int32
U32 = mybir.dt.uint32
U16 = mybir.dt.uint16
U8 = mybir.dt.uint8
FP8X4 = mybir.dt.float8_e4m3fn_x4
COPY = mybir.ActivationFunctionType.Copy
IDENTITY = mybir.ActivationFunctionType.Identity
ADD = mybir.AluOpType.add
MULT = mybir.AluOpType.mult

K, T, N = 2048, 256, 256
P = 128
PASSES = 4
FLOPS = 2 * K * T * N


def tile_picked_actorder_lin_bias_perm_l_kernel(tc, x, w_words, w_scales, b, offs, out):
    nc = tc.nc
    with ExitStack() as ctx:
        keep = ctx.enter_context(tc.tile_pool(name="keep", bufs=1))
        ring = ctx.enter_context(tc.tile_pool(name="ring", bufs=8))
        turned = ctx.enter_context(tc.psum_pool(name="turned", bufs=4))
        sums = ctx.enter_context(tc.psum_pool(name="sums", bufs=1))

        offsets = keep.tile([P, K // 16], U16, name="offsets")
        x32 = [keep.tile([P, K], F32, name="x32_%d" % h) for h in range(2)]
        x16 = [keep.tile([P, K], BF16, name="x16_%d" % h) for h in range(2)]
        w_codes = keep.tile([P, PASSES, N], U32, name="w_codes", align_bytes=64)
        w_planes = keep.tile([P, N], U8, name="w_planes", align_bytes=64)
        bias = keep.tile([P, 2], F32, name="bias")
        ident = keep.tile([P, P], F32, name="ident")

        def load_x(h, lo, hi):
            nc.sync.dma_start(x32[h][:, lo:hi], x[P * h : P * h + P, lo:hi])

        make_identity(nc, ident[:])
        nc.vector.memset(w_planes[:].bitcast(I32), 0)

        load_x(0, 0, 512)
        load_x(0, 512, 1024)
        nc.sync.dma_start(offsets[:], offs)
        load_x(0, 1024, 1536)
        load_x(0, 1536, 2048)
        load_x(1, 0, 2048)
        nc.sync.dma_start(w_codes[:].bitcast(I32), w_words.rearrange("a p n t -> p a (n t)").bitcast(I32))
        for q in range(4):
            nc.sync.dma_start(
                w_planes[32 * q : 32 * q + 16, :].bitcast(I32), w_scales[:, 4 * q : 4 * q + 4, :].bitcast(I32)
            )
        nc.sync.dma_start(bias[:], b.rearrange("(c p) o -> p (c o)", p=P))

        acc = [[sums.tile([P, P], F32, name="acc_%d_%d" % (h, m)) for m in range(2)] for h in range(2)]
        gathered = {}
        place = {}
        words = {}
        grouped = {}
        codes = {}
        planes = {}
        seen = [0, 0]

        def cast(h, lo, hi, engine):
            if engine == "v":
                nc.vector.tensor_copy(x16[h][:, lo:hi], x32[h][:, lo:hi])
            elif engine == "g":
                nc.gpsimd.tensor_scalar(x16[h][:, lo:hi], x32[h][:, lo:hi], 1.0, 0.0, MULT, ADD)
            else:
                nc.scalar.copy(x16[h][:, lo:hi], x32[h][:, lo:hi])

        def gather(h, a, engine):
            g = ring.tile([P, 2, 256], BF16, name="g", align_bytes=64)
            gathered[h, a] = g
            dst = g[:].rearrange("p u (j e) -> p j u e", e=2)
            picks = offsets[:, 32 * a : 32 * a + 32]
            if engine == "v":
                nc.vector.tensor_copy(dst, x32[h][:].indirect(picks))
            else:
                nc.scalar.activation(dst, x16[h][:].indirect(picks), COPY)

        groups = {(1, 1): [(1, 1)], (1, 2): [(1, 2), (0, 3)], (0, 2): [(0, 2)], (0, 1): [(0, 1), (0, 0)], (1, 0): [(1, 0)], (1, 3): [(1, 3)]}
        for lead, members in groups.items():
            for i, unit in enumerate(members):
                place[unit] = (lead, i)

        def turn(h, a):
            lead, i = place[h, a]
            if lead not in words:
                w = turned.tile([P, 2, 2, P], F32, name="xt")
                words[lead] = w
            pairs = gathered[h, a][:].rearrange("p u w -> p (u w)").bitcast(F32)
            for u in range(2):
                nc.tensor.transpose(words[lead][:, i, u, :], pairs[:, P * u : P * u + P], ident[:])

        def regroup(h, a, engine):
            n = len(groups[h, a])
            q = ring.tile([P, n, 4 * P], BF16, name="q%d" % n, align_bytes=64)
            grouped[h, a] = q
            dst = q[:].rearrange("p n w -> p (n w)").bitcast(F32).rearrange("p (n r u) -> p n r u", n=n, u=2)
            src = words[h, a][:, 0:n, :, :].rearrange("p n u r -> p n r u")
            if engine == "v":
                nc.vector.tensor_copy(dst, src)
            else:
                nc.scalar.copy(dst, src)

        def quant(h, a):
            n = len(groups[h, a])
            c = ring.tile([P, n, P], U32, name="codes%d" % n, align_bytes=64)
            s = ring.tile([P, n, P], U8, name="planes%d" % n, align_bytes=64)
            codes[h, a] = c
            planes[h, a] = s
            nc.vector.quantize_mx(
                out=c[:].rearrange("p n r -> p (n r)").bitcast(FP8X4),
                scales=s[:].rearrange("p n r -> p (n r)"),
                in_=grouped[h, a][:].rearrange("p n w -> p (n w)"),
            )

        def mult(h, a):
            lead, i = place[h, a]
            for m in range(2):
                rows = slice(P * m, P * m + P)
                nc.tensor.matmul_mx(
                    out=acc[h][m][:],
                    lhsT=w_codes[:, a, rows].bitcast(FP8X4),
                    lhsT_scale=w_planes[4 * a : P, rows],
                    rhs=codes[lead][:, i, :].bitcast(FP8X4),
                    rhs_scale=planes[lead][:, i, :],
                    start=(seen[h] == 0),
                    stop=(seen[h] == PASSES - 1),
                )
            seen[h] += 1

        def store(h, m, engine, queue):
            o = ring.tile([P, P], F32, name="o")
            if engine == "v":
                nc.vector.tensor_scalar(o[:], acc[h][m][:], bias[:, m : m + 1], None, ADD)
            else:
                nc.scalar.activation(o[:], acc[h][m][:], IDENTITY, bias=bias[:, m : m + 1])
            queue.dma_start(out[P * m : P * m + P, P * h : P * h + P], o[:])

        cast(0, 0, 512, "v")
        cast(0, 512, 1024, "s")
        cast(0, 1024, 1536, "v")
        gather(0, 3, "v")
        cast(0, 1536, 2048, "s")
        gather(0, 1, "s")
        turn(0, 3)
        gather(0, 2, "s")
        gather(1, 0, "v")
        turn(0, 1)
        gather(0, 0, "s")
        gather(1, 2, "v")
        turn(0, 2)
        turn(1, 0)
        gather(1, 3, "v")
        regroup(1, 0, "s")
        turn(0, 0)
        regroup(0, 2, "s")
        regroup(0, 1, "s")
        turn(1, 2)
        gather(1, 1, "v")
        turn(1, 3)
        regroup(1, 2, "s")
        regroup(1, 3, "s")
        quant(0, 1)
        turn(1, 1)
        quant(1, 2)
        mult(0, 0)
        mult(0, 1)
        quant(0, 2)
        regroup(1, 1, "s")
        mult(1, 2)
        quant(1, 3)
        mult(0, 3)
        quant(1, 0)
        mult(0, 2)
        quant(1, 1)
        mult(1, 3)
        mult(1, 0)
        store(0, 0, "v", nc.sync)
        store(0, 1, "s", nc.scalar)
        mult(1, 1)
        store(1, 0, "v", nc.sync)
        store(1, 1, "s", nc.scalar)
